import numpy as np
import ml_dtypes


def mxq(x, axis, fmt="e4m3"):
    dtype, down = {"e4m3": (ml_dtypes.float8_e4m3fn, 7), "e5m2": (ml_dtypes.float8_e5m2, 14)}[fmt]
    v = np.moveaxis(np.asarray(x, np.float32).astype(ml_dtypes.bfloat16).astype(np.float64), axis, -1)
    blocks = v.reshape(v.shape[:-1] + (-1, 32))
    amax = np.abs(blocks).max(-1, keepdims=True)
    byte = np.maximum(np.where(amax > 0, np.frexp(amax)[1] - 1 + 127, 0) - down, 1)
    scale = np.exp2(byte - 127.0)
    codes = (blocks / scale).astype(np.float32).astype(dtype).astype(np.float64)
    return np.moveaxis((codes * scale).reshape(v.shape), -1, axis)


WIDE = False


def mx_kscale(k):
    if not WIDE:
        return np.ones(k)
    levels = np.array([10, -10, 5, -5, 0])
    if k % 512:
        return np.exp2(np.random.permutation(np.resize(levels, k // 32))).repeat(32)
    a = np.empty((k // 512, 16))
    for p in range(k // 512):
        a[p, :8] = np.random.permutation(np.resize(levels, 8))
        for g in range(8):
            far = levels[np.abs(levels - a[p, g]) >= 10]
            a[p, g + 8] = far[np.random.randint(len(far))]
    return np.exp2(a.ravel()).repeat(32)


BF16 = ml_dtypes.bfloat16


def bf(x):
    return np.asarray(x, np.float32).astype(BF16)


def f64(x):
    return np.asarray(x).astype(np.float64)


E2M1 = np.array([0.0, 0.5, 1.0, 1.5, 2.0, 3.0, 4.0, 6.0, -0.0, -0.5, -1.0, -1.5, -2.0, -3.0, -4.0, -6.0])


def pack_weight(w, fmt):
    k, n = w.shape
    w = f64(bf(w)).reshape(k // 32, 32, n)
    amax = np.abs(w).max(1)
    if fmt == "e4m3":
        byte = np.frexp(amax)[1] - 1 + 127 - 7
    else:
        mant, ex = np.frexp(amax / 6.0)
        byte = np.where(mant > 0.5, ex, ex - 1) + 127
    byte = np.clip(np.where(amax > 0, byte, 1), 1, 254)
    scaled = (w * np.exp2(127.0 - byte)[:, None, :]).reshape(k, n).astype(np.float32)
    by_word = np.ascontiguousarray(scaled.reshape(k // 512, 128, 4, n).transpose(0, 1, 3, 2))
    if fmt == "e4m3":
        words = by_word.astype(ml_dtypes.float8_e4m3fn).view(np.uint8)
    else:
        c = by_word.astype(ml_dtypes.float4_e2m1fn).view(np.uint8) & 0xF
        words = c[..., 0::2] | (c[..., 1::2] << 4)
    return np.ascontiguousarray(words), np.ascontiguousarray(byte.astype(np.uint8).reshape(k // 512, 16, n))


def unpack_weight(words, scales, fmt):
    g, p, n, _ = words.shape
    if fmt == "e4m3":
        vals = np.ascontiguousarray(words).view(ml_dtypes.float8_e4m3fn).astype(np.float64)
    else:
        nib = np.empty((g, p, n, 4), np.uint8)
        nib[..., 0::2] = words & 0xF
        nib[..., 1::2] = words >> 4
        vals = E2M1[nib]
    vals = vals * np.repeat(np.exp2(scales.astype(np.float64) - 127.0), 8, axis=1)[..., None]
    return vals.transpose(0, 1, 3, 2).reshape(g * 512, n)
def pack4(w):
    words, scales = pack_weight(w, "e2m1")
    return words.reshape(words.shape[0], 128, -1), scales


def unpack4(words, scales):
    return unpack_weight(words.reshape(words.shape[0], 128, -1, 2), scales, "e2m1")


def planes(Y):
    n, m = Y.shape
    b = f64(bf(Y)).reshape(n // 32, 32, m)
    amax = np.abs(b).max(1)
    byte = np.clip(np.where(amax > 0, np.frexp(amax)[1] - 1 + 127 - 7, 1), 1, 254)
    codes = (b * np.exp2(127.0 - byte)[:, None, :]).reshape(n, m).astype(np.float32).astype(ml_dtypes.float8_e4m3fn).view(np.uint8)
    words = codes.reshape(n // 512, 128, 4, m).transpose(0, 1, 3, 2)
    return np.ascontiguousarray(words), np.ascontiguousarray(byte.astype(np.uint8).reshape(n // 512, 16, m))


NT, NC, NS, NP, NF = 1024, 1536, 2048, 512, 8

def panel(F, width):
    L = np.random.randn(NF, width)
    G = 0.45 * np.random.randn(NS, width)
    for j in range(NF):
        G = G + 0.9 / np.sqrt(NF) * F[:, j:j + 1] * L[j:j + 1, :]
    return G

def setup_inputs():
    s = mx_kscale(NS)
    t = mx_kscale(NC)
    F = np.random.randn(NS, NF)
    gt_words, gt_scales = pack4(panel(F, NT) * s[:, None])
    gc_words, gc_scales = pack4(panel(F, NC) * t[None, :] / s[:, None])
    incl = 1.0 / (1.0 + np.exp(1.0 - 1.5 * np.random.randn(NC, NP)))
    mu = 10.0 / np.sqrt(NC) * np.random.randn(NC, NP) / t[:, None]
    z = 1.5 * np.random.randn(NT, NP)
    w = np.exp(0.8 * np.random.randn(NT))
    return {"gt_words": gt_words, "gt_scales": gt_scales, "gc_words": gc_words, "gc_scales": gc_scales,
            "incl": bf(incl), "mu": bf(mu), "z": bf(z), "w": bf(w)}

def reference(gt_words, gt_scales, gc_words, gc_scales, incl, mu, z, w):
    Gt = unpack4(gt_words, gt_scales)
    Gc = unpack4(gc_words, gc_scales)
    R = (Gt.T @ Gc) / NS
    b = f64(incl) * f64(mu)
    fit = mxq(R, 1) @ mxq(b, 0)
    y = (f64(z) - fit) * f64(w)[:, None]
    words, scales = planes(y)
    return y, words, scales

from contextlib import ExitStack

import concourse.mybir as mybir

NT, NC, NS, NP = 1024, 1536, 2048, 512
FLOPS = 2 * NT * NC * NS + 2 * NT * NC * NP

F32 = mybir.dt.float32
BF16 = mybir.dt.bfloat16
I32 = mybir.dt.int32
U32 = mybir.dt.uint32
U8 = mybir.dt.uint8
FP4X4 = mybir.dt.float4_e2m1fn_x4
FP8X4 = mybir.dt.float8_e4m3fn_x4
ALU = mybir.AluOpType
COPY = mybir.ActivationFunctionType.Copy

P = 128
PACK = 4
GROUP = P * PACK
SAMPLE_PASSES = NS // GROUP
CAND_GROUPS = NC // GROUP
TARGET_GROUPS = NT // GROUP
HALF = NP // 2
QUARTER = NP // 4
SLOTS_PER_BANK = [1, 1, 1, 1, 1, 2]


def tile_fine_mapping_residual_k5_kernel(
    tc, gt_words, gt_scales, gc_words, gc_scales, incl, mu, z, w, out_0, out_1, out_2
):
    nc = tc.nc
    with ExitStack() as ctx:
        sb = ctx.enter_context(tc.tile_pool(name="sb", bufs=1))
        ps = ctx.enter_context(tc.psum_pool(name="ps", bufs=1))
        ctx.enter_context(tc.manual_schedule())

        def tiles(name, count, shape, dtype):
            return [sb.tile(shape, dtype, name="%s%d" % (name, i), align_bytes=256) for i in range(count)]

        banks = [ps.tile([P, GROUP], F32, name="bank%d" % i) for i in range(8)]
        gt_codes = tiles("gt_codes", TARGET_GROUPS, [P, SAMPLE_PASSES, 2 * GROUP], U8)
        gt_plane = tiles("gt_plane", TARGET_GROUPS, [P, SAMPLE_PASSES, GROUP], U8)
        gc_raw = tiles("gc_raw", CAND_GROUPS, [P, SAMPLE_PASSES, 2 * GROUP], U8)
        gc_codes = tiles("gc_codes", CAND_GROUPS, [P, SAMPLE_PASSES, 2 * GROUP], U8)
        gc_rows_first = sb.tile([P, SAMPLE_PASSES, GROUP], U8, name="gc_rows_first", align_bytes=256)
        gc_rows_rest = sb.tile([P, SAMPLE_PASSES, 2 * GROUP], U8, name="gc_rows_rest", align_bytes=256)
        gc_rows = [gc_rows_first[:], gc_rows_rest[:, :, :GROUP], gc_rows_rest[:, :, GROUP:]]
        gc_plane = tiles("gc_plane", CAND_GROUPS, [P, SAMPLE_PASSES, GROUP], U8)
        incl_sb = tiles("incl_sb", CAND_GROUPS, [P, PACK, NP], BF16)
        mu_sb = tiles("mu_sb", CAND_GROUPS, [P, PACK, NP], BF16)
        b_rows = tiles("b_rows", CAND_GROUPS, [P, PACK, NP], BF16)
        b_packed = tiles("b_packed", CAND_GROUPS, [P, NP, PACK], BF16)
        b_codes = tiles("b_codes", CAND_GROUPS, [P, NP], U32)
        b_plane = tiles("b_plane", CAND_GROUPS, [P, NP], U8)
        r_stage = tiles("r_stage", 3, [P, PACK * GROUP], BF16)
        r_packed = tiles("r_packed", 3, [P, GROUP, PACK], BF16)
        r_codes = tiles("r_codes", 6, [P, GROUP], U32)
        r_plane = tiles("r_plane", 6, [P, GROUP], U8)
        z_sb = tiles("z_sb", TARGET_GROUPS, [P, PACK, NP], BF16)
        zw = tiles("zw", TARGET_GROUPS, [P, PACK, NP], F32)
        y = tiles("y", TARGET_GROUPS, [P, PACK, NP], F32)
        y_packed = tiles("y_packed", TARGET_GROUPS, [P, NP, PACK], BF16)
        y_codes = tiles("y_codes", TARGET_GROUPS, [P, NP], U32)
        y_plane = tiles("y_plane", TARGET_GROUPS, [P, NP], U8)
        w_sb = sb.tile([P, TARGET_GROUPS, PACK], BF16, name="w_sb", align_bytes=256)
        w_pos = sb.tile([P, TARGET_GROUPS, PACK], F32, name="w_pos", align_bytes=256)
        w_neg = sb.tile([P, TARGET_GROUPS, PACK], F32, name="w_neg", align_bytes=256)

        gt_w = gt_words.bitcast(I32).rearrange("k p n -> p k n")
        gc_w = gc_words.bitcast(I32).rearrange("k p n -> p k n")
        gt_s = gt_scales.bitcast(I32).rearrange("k (q r) n -> r q k n", r=4)
        gc_s = gc_scales.bitcast(I32).rearrange("k (q r) n -> r q k n", r=4)

        def load_words(dst, src, group, passes):
            nc.sync.dma_start(
                out=dst[:, passes, :].bitcast(I32), in_=src[:, passes, 256 * group : 256 * (group + 1)]
            )

        def load_scale_rows(dst, src, first_col, cols):
            for r in range(4):
                nc.sync.dma_start(
                    out=dst[r:P:32, :, :].bitcast(I32), in_=src[r][:, :, first_col // 4 : (first_col + cols) // 4]
                )

        def load_effects(g):
            rows = slice(GROUP * g, GROUP * (g + 1))
            for src, dst in ((incl, incl_sb[g]), (mu, mu_sb[g])):
                by_slot = src[rows, :].rearrange("(q j r) m -> j q r m", j=PACK, r=8)
                for j in range(PACK):
                    nc.sync.dma_start(out=dst[:, j, :], in_=by_slot[j])

        def permute_words(g, passes):
            nc.vector.tensor_copy(
                out=gc_codes[g][:, passes, :].bitcast(I32).rearrange("p k (j q c) -> p k j q c", j=PACK, c=4),
                in_=gc_raw[g][:, passes, :].bitcast(I32).rearrange("p k (q j c) -> p k j q c", j=PACK, c=4),
            )

        def permute_scales(g):
            nc.vector.tensor_copy(
                out=gc_plane[g][:].bitcast(I32).rearrange("p k (j q c) -> p k j q c", j=PACK, c=2),
                in_=gc_rows[g].bitcast(I32).rearrange("p k (q j c) -> p k j q c", j=PACK, c=2),
            )

        def chunk_banks(c):
            return banks[4 * (c % 2) : 4 * (c % 2) + 4] if c < 4 else banks[4 * ((c + 1) % 2) : 4 * ((c + 1) % 2) + 4]

        def ld_pass(c, i, e, k):
            h, g = divmod(c, CAND_GROUPS)
            per_bank = SLOTS_PER_BANK[c]
            width = GROUP // per_bank
            part, u = divmod(i, PACK // per_bank)
            j = per_bank * u + e
            n0 = width * part
            nc.tensor.matmul_mx(
                out=chunk_banks(c)[i][:, width * e : width * (e + 1)],
                lhsT=gc_codes[g][:, k, 2 * P * j : 2 * P * (j + 1)].bitcast(FP4X4),
                lhsT_scale=gc_plane[g][:, k, P * j : P * (j + 1)],
                rhs=gt_codes[h][:, k, 2 * n0 : 2 * (n0 + width)].bitcast(FP4X4),
                rhs_scale=gt_plane[h][:, k, n0 : n0 + width],
                start=(k == 0),
                stop=(k == SAMPLE_PASSES - 1),
            )

        def ld_chunk(c):
            for i in range(4):
                for e in range(SLOTS_PER_BANK[c]):
                    for k in range(SAMPLE_PASSES):
                        ld_pass(c, i, e, k)

        def stage_view(c):
            per_bank = SLOTS_PER_BANK[c]
            return r_stage[c % 3][:].rearrange("p (u t m e) -> p u t m e", t=PACK, m=P, e=per_bank)

        def drain_ld(c, i):
            per_bank = SLOTS_PER_BANK[c]
            part, u = divmod(i, PACK // per_bank)
            rows = P // per_bank
            nc.scalar.activation(
                out=stage_view(c)[:, u, :, rows * part : rows * (part + 1), :],
                in_=chunk_banks(c)[i][:].rearrange("p (e m t) -> p t m e", e=per_bank, t=PACK),
                func=COPY,
                scale=1.0 / NS,
            )

        def pack_r(c):
            if SLOTS_PER_BANK[c] == 1:
                nc.vector.tensor_copy(
                    out=r_packed[c % 3][:].rearrange("p (n i) j -> p n j i", i=4),
                    in_=r_stage[c % 3][:].rearrange("p (j n i) -> p n j i", j=PACK, i=4),
                )
            else:
                nc.vector.tensor_copy(
                    out=r_packed[c % 3][:].rearrange("p n (u e) -> p n u e", e=2),
                    in_=r_stage[c % 3][:].rearrange("p (u n e) -> p n u e", u=2, e=2),
                )

        def pack_r_part(c, slots, part):
            rows = slice(64 * part, 64 * (part + 1))
            nc.vector.tensor_copy(
                out=r_packed[c % 3][:].rearrange("p (t m) (u e) -> p t m u e", t=PACK, e=2)[:, slots, rows, :, :],
                in_=stage_view(c).rearrange("p u t m e -> p t m u e")[:, slots, rows, :, :],
            )

        def quantize(codes, plane, packed, cols):
            nc.vector.quantize_mx(
                out=codes[:, cols].bitcast(FP8X4),
                scales=plane[:, cols],
                in_=packed[:, cols, :].rearrange("p n j -> p (n j)"),
            )

        def quantize_r(c, cols=slice(0, GROUP)):
            quantize(r_codes[c], r_plane[c], r_packed[c % 3], cols)

        def quantize_b(g):
            quantize(b_codes[g], b_plane[g], b_packed[g], slice(0, NP))

        def quantize_y(h, cols):
            quantize(y_codes[h], y_plane[h], y_packed[h], cols)

        def multiply_effects(g):
            nc.vector.tensor_tensor(out=b_rows[g][:], in0=incl_sb[g][:], in1=mu_sb[g][:], op=ALU.mult)

        def pack_views(packed, rows, cols):
            return dict(
                out=packed[:, cols, :].rearrange("p (n i) j -> p n j i", i=4),
                in_=rows[:, :, cols].rearrange("p j (n i) -> p n j i", i=4),
            )

        def quarter(i):
            return slice(QUARTER * i, QUARTER * (i + 1))

        def half(i):
            return slice(HALF * i, HALF * (i + 1))

        def pack_b_scalar(g, i):
            nc.scalar.copy(**pack_views(b_packed[g], b_rows[g], quarter(i)))

        def fit_banks(h):
            return banks[4 * h : 4 * h + 4]

        def fit_passes(h, g):
            c = CAND_GROUPS * h + g
            for t in range(PACK):
                cols = slice(P * t, P * (t + 1))
                nc.tensor.matmul_mx(
                    out=fit_banks(h)[t][:],
                    lhsT=r_codes[c][:, cols].bitcast(FP8X4),
                    lhsT_scale=r_plane[c][:, cols],
                    rhs=b_codes[g][:].bitcast(FP8X4),
                    rhs_scale=b_plane[g][:],
                    start=(g == 0),
                    stop=(g == CAND_GROUPS - 1),
                )

        def weight_z(h, t):
            nc.scalar.activation(out=zw[h][:, t, :], in_=z_sb[h][:, t, :], func=COPY, scale=w_pos[:, h, t : t + 1])

        def residual(h, t, cols):
            nc.vector.scalar_tensor_tensor(
                out=y[h][:, t, cols],
                in0=fit_banks(h)[t][:, cols],
                scalar=w_neg[:, h, t : t + 1],
                in1=zw[h][:, t, cols],
                op0=ALU.mult,
                op1=ALU.add,
            )

        def store_y(h, cols):
            rows = out_0[GROUP * h : GROUP * (h + 1), :].rearrange("(p t) m -> p t m", t=PACK)
            nc.sync.dma_start(out=rows[:, :, cols], in_=y[h][:, :, cols])

        def store_codes(h, cols):
            words = out_1[h].rearrange("p m t -> p (m t)").bitcast(I32)
            nc.sync.dma_start(out=words[:, cols], in_=y_codes[h][:, cols].bitcast(I32))

        def store_scales(h, queues):
            for q in range(4):
                queues[q].dma_start(
                    out=out_2[h, 4 * q : 4 * q + 4, :].bitcast(I32),
                    in_=y_plane[h][32 * q : 32 * q + 4, :].bitcast(I32),
                )

        everything = slice(0, NP)
        first, rest, all_passes = slice(0, 1), slice(1, SAMPLE_PASSES), slice(0, SAMPLE_PASSES)

        for plane in (gc_rows_first, gt_plane[0], gc_rows_rest, gt_plane[1]):
            nc.vector.memset(plane[:].bitcast(I32), 0)

        load_words(gc_raw[0], gc_w, 0, first)
        load_words(gt_codes[0], gt_w, 0, first)
        load_scale_rows(gc_rows_first, gc_s, 0, GROUP)
        load_scale_rows(gt_plane[0], gt_s, 0, GROUP)
        load_words(gc_raw[0], gc_w, 0, rest)
        load_words(gt_codes[0], gt_w, 0, rest)
        load_scale_rows(gc_rows_rest, gc_s, GROUP, 2 * GROUP)
        load_words(gc_raw[1], gc_w, 1, all_passes)
        load_effects(0)
        load_words(gc_raw[2], gc_w, 2, all_passes)
        load_effects(1)
        load_scale_rows(gt_plane[1], gt_s, GROUP, GROUP)
        load_words(gt_codes[1], gt_w, 1, all_passes)
        load_effects(2)
        nc.sync.dma_start(out=w_sb[:], in_=w.rearrange("(h p t) -> p h t", p=P, t=PACK))
        for h in range(TARGET_GROUPS):
            nc.sync.dma_start(
                out=z_sb[h][:], in_=z[GROUP * h : GROUP * (h + 1), :].rearrange("(p t) m -> p t m", t=PACK)
            )

        permute_words(0, first)
        permute_scales(0)
        for k in range(1, SAMPLE_PASSES):
            permute_words(0, slice(k, k + 1))
        for k in range(SAMPLE_PASSES):
            for i in range(4):
                ld_pass(0, i, 0, k)

        permute_scales(1)
        permute_scales(2)
        permute_words(1, all_passes)
        ld_chunk(1)
        for i in range(4):
            drain_ld(0, i)
        drain_ld(1, 0)
        drain_ld(1, 1)

        multiply_effects(0)
        permute_words(2, all_passes)
        pack_r(0)
        pack_b_scalar(0, 0)
        drain_ld(1, 2)
        drain_ld(1, 3)
        ld_chunk(2)
        quantize_r(0)
        multiply_effects(1)
        pack_r(1)
        quantize_r(1)
        for i in range(3):
            pack_b_scalar(0, i + 1)
            drain_ld(2, i)
        pack_b_scalar(1, 0)
        drain_ld(2, 3)

        ld_chunk(3)
        quantize_b(0)
        multiply_effects(2)
        pack_r(2)
        nc.vector.tensor_copy(**pack_views(b_packed[2], b_rows[2], everything))
        quantize_r(2)
        for i in range(3):
            pack_b_scalar(1, i + 1)
            drain_ld(3, i)
        nc.scalar.activation(out=w_pos[:], in_=w_sb[:], func=COPY)
        nc.scalar.activation(out=w_neg[:], in_=w_sb[:], func=COPY, scale=-1.0)
        weight_z(0, 0)
        drain_ld(3, 3)
        for t in range(1, PACK):
            weight_z(0, t)
        weight_z(1, 0)
        weight_z(1, 1)

        quantize_b(1)
        quantize_b(2)
        for g in range(CAND_GROUPS):
            fit_passes(0, g)
        ld_chunk(4)
        pack_r(3)
        residual(0, 0, everything)
        quantize_r(3)
        for t in range(1, PACK):
            residual(0, t, everything)
        store_y(0, everything)

        for i in range(2):
            drain_ld(4, i)
            nc.scalar.copy(**pack_views(y_packed[0], y[0], half(i)))
        drain_ld(4, 2)
        drain_ld(4, 3)
        ld_chunk(5)
        pack_r(4)
        quantize_y(0, everything)
        quantize_r(4)
        store_codes(0, everything)
        store_scales(0, [nc.sync] * 4)

        for i in range(2):
            drain_ld(5, i)
            weight_z(1, 2 + i)
        pack_r_part(5, slice(0, PACK), 0)
        drain_ld(5, 2)
        drain_ld(5, 3)
        fit_passes(1, 0)
        fit_passes(1, 1)
        pack_r_part(5, slice(0, 1), 1)
        for t in range(PACK):
            if t + 1 < PACK:
                pack_r_part(5, slice(t + 1, t + 2), 1)
            quantize_r(5, slice(P * t, P * (t + 1)))
        fit_passes(1, 2)

        for t in range(PACK):
            residual(1, t, half(0))
        store_y(1, half(0))
        nc.scalar.copy(**pack_views(y_packed[1], y[1], half(0)))
        for t in range(PACK):
            residual(1, t, half(1))
        store_y(1, half(1))
        nc.vector.tensor_copy(**pack_views(y_packed[1], y[1], half(1)))
        quantize_y(1, half(0))
        store_codes(1, half(0))
        quantize_y(1, half(1))
        store_codes(1, half(1))
        store_scales(1, [nc.sync, nc.scalar, nc.sync, nc.scalar])
